import numpy as np
import ml_dtypes


def mxq(x, axis, fmt="e4m3"):
    dtype, down = {"e4m3": (ml_dtypes.float8_e4m3fn, 7), "e5m2": (ml_dtypes.float8_e5m2, 14)}[fmt]
    v = np.moveaxis(np.asarray(x, np.float32).astype(ml_dtypes.bfloat16).astype(np.float64), axis, -1)
    blocks = v.reshape(v.shape[:-1] + (-1, 32))
    amax = np.abs(blocks).max(-1, keepdims=True)
    byte = np.maximum(np.where(amax > 0, np.frexp(amax)[1] - 1 + 127, 0) - down, 1)
    scale = np.exp2(byte - 127.0)
    codes = (blocks / scale).astype(np.float32).astype(dtype).astype(np.float64)
    return np.moveaxis((codes * scale).reshape(v.shape), -1, axis)


WIDE = False


def mx_kscale(k):
    if not WIDE:
        return np.ones(k)
    levels = np.array([10, -10, 5, -5, 0])
    if k % 512:
        return np.exp2(np.random.permutation(np.resize(levels, k // 32))).repeat(32)
    a = np.empty((k // 512, 16))
    for p in range(k // 512):
        a[p, :8] = np.random.permutation(np.resize(levels, 8))
        for g in range(8):
            far = levels[np.abs(levels - a[p, g]) >= 10]
            a[p, g + 8] = far[np.random.randint(len(far))]
    return np.exp2(a.ravel()).repeat(32)


def f64(x):
    return np.asarray(x).astype(np.float64)


def striped(idx):
    return np.tile(idx.reshape(-1, 16).T, (8, 1)).astype(np.uint16)


def unstriped(offs):
    return offs[:16].T.reshape(-1).astype(np.int64)


def striped8(idx):
    return np.concatenate([x.reshape(-1, 16).T for x in idx]).astype(np.uint16)


def runs(offs, k):
    lists = np.stack([offs[16 * r : 16 * r + 16].T.reshape(-1) for r in range(8)]).astype(np.int64)
    return lists[np.arange(k) % 512 // 64]


def pack_weight(w):
    k, n = w.shape
    w = f64(np.asarray(w, np.float32).astype(ml_dtypes.bfloat16)).reshape(k // 32, 32, n)
    amax = np.abs(w).max(1)
    byte = np.clip(np.where(amax > 0, np.frexp(amax)[1] - 1 + 127 - 7, 1), 1, 254)
    scaled = (w * np.exp2(127.0 - byte)[:, None, :]).reshape(k, n).astype(np.float32)
    words = np.ascontiguousarray(scaled.reshape(k // 512, 128, 4, n).transpose(0, 1, 3, 2)).astype(ml_dtypes.float8_e4m3fn).view(np.uint8)
    return words, np.ascontiguousarray(byte.astype(np.uint8).reshape(k // 512, 16, n))


def unpack_weight(words, scales):
    g, p, n, _ = words.shape
    vals = np.ascontiguousarray(words).view(ml_dtypes.float8_e4m3fn).astype(np.float64) * np.repeat(np.exp2(scales.astype(np.float64) - 127.0), 8, axis=1)[..., None]
    return vals.transpose(0, 1, 3, 2).reshape(g * 512, n)


def sigmoid(v):
    return 1.0 / (1.0 + np.exp(-np.maximum(v, -700.0)))


K, T, S, N, H, U = 512, 2048, 512, 512, 512, 1024


def setup_inputs():
    n = np.random.standard_normal
    s = mx_kscale(K)[:, None]
    u = mx_kscale(H)
    packed_xT = pack_weight(n((K, T)) * s)
    return {
        "x_words": packed_xT[0],
        "x_scales": packed_xT[1],
        "w1": (n((K, H)) / np.sqrt(K) / s).astype(np.float32),
        "w2": (n((K, H)) / np.sqrt(K) / s).astype(np.float32),
        "tel": n((H, S)).astype(np.float32),
        "gn": (np.random.uniform(0.5, 1.5, (H, 1)) * u[:, None]).astype(np.float32),
        "w3": (n((H, N)) / np.sqrt(H) / u[:, None]).astype(np.float32),
        "mem": n((N, U)).astype(np.float32),
        "offs": striped(np.random.permutation(T)[:S]),
        "two": striped(np.random.permutation(T)[:S]),
        "in1": striped8(np.stack([np.random.permutation(S) for _ in range(8)])),
        "in2": striped8(np.stack([np.random.permutation(S) for _ in range(8)])),
        "slot": striped8(np.stack([np.random.permutation(U)[:S] for _ in range(8)])),
    }


def reference(x_words, x_scales, w1, w2, tel, gn, w3, mem, offs, two, in1, in2, slot):
    xq = unpack_weight(x_words, x_scales)[:, unstriped(offs)]
    y = mxq(f64(w1), 0, "e4m3").T @ xq
    x_two = unpack_weight(x_words, x_scales)[:, unstriped(two)]
    c = sigmoid(mxq(f64(w2), 0, "e4m3").T @ x_two)
    sh = y / (c + 0.25)
    z = f64(gn) * (0.5 * (sh[np.arange(H)[:, None], runs(in1, H)] + sh[np.arange(H)[:, None], runs(in2, H)]) + 0.5 * f64(tel))
    h = mxq(f64(w3), 0, "e4m3").T @ mxq(z, 0, "e4m3")
    out = f64(mem).copy()
    out[np.arange(N)[:, None], runs(slot, N)] = h
    return out

@@ -1,0 +1,237 @@
+import math
+from contextlib import ExitStack
+
+import concourse.mybir as mybir
+
+K, T, S, N, H, U = 512, 2048, 512, 512, 512, 1024
+FLOPS = 2 * K * H * S * 2 + 2 * H * N * S
+
+F32 = mybir.dt.float32
+BF16 = mybir.dt.bfloat16
+I32 = mybir.dt.int32
+U32 = mybir.dt.uint32
+U16 = mybir.dt.uint16
+U8 = mybir.dt.uint8
+FP8X4 = mybir.dt.float8_e4m3fn_x4
+ACT = mybir.ActivationFunctionType
+ALU = mybir.AluOpType
+
+P = 128
+PACK = 4
+CHUNKS = 2
+CW = S // CHUNKS
+LW = CW // 16
+W2_SCALAR_COLS = 128
+W1_SCALAR_COLS = 32
+
+
+def tile_picked_rankstep_none_p_kernel(
+    tc, x_words, x_scales, w1, w2, tel, gn, w3, mem, offs, two, in1, in2, slot, out
+):
+    nc = tc.nc
+    with ExitStack() as ctx:
+        lists = ctx.enter_context(tc.tile_pool(name="lists", bufs=1))
+        keep = ctx.enter_context(tc.tile_pool(name="keep", bufs=1))
+        psum = ctx.enter_context(tc.psum_pool(name="psum", bufs=1))
+
+        def load_list(src, name):
+            tile = lists.tile([P, S // 16], U16, name=name)
+            nc.sync.dma_start(tile[:], src)
+            return tile
+
+        def load_weight(w, name):
+            raw = keep.tile([P, PACK, H], F32, name=name)
+            nc.sync.dma_start(raw[:], w.rearrange("(p j) c -> p j c", j=PACK))
+            return raw
+
+        def load_rows(src, t, name):
+            tile = keep.tile([P, src.shape[1]], F32, name=name)
+            nc.sync.dma_start(tile[:], src.rearrange("(p t) c -> p t c", t=PACK)[:, t, :])
+            return tile
+
+        table_scales = keep.tile([P, T], U8, name="table_scales")
+        nc.gpsimd.memset(table_scales[:].bitcast(I32), 0)
+        two_list = load_list(two, "two_list")
+        offs_list = load_list(offs, "offs_list")
+        for q in range(4):
+            nc.gpsimd.dma_start(
+                table_scales[32 * q : 32 * q + 4, :].bitcast(I32),
+                x_scales[0, 4 * q : 4 * q + 4, :].bitcast(I32),
+            )
+        table_words = keep.tile([P, T], U32, name="table_words")
+        nc.sync.dma_start(table_words[:].bitcast(I32), x_words[0].rearrange("p c r -> p (c r)").bitcast(I32))
+        w2_raw = load_weight(w2, "w2_raw")
+        w1_raw = load_weight(w1, "w1_raw")
+        in1_list = load_list(in1, "in1_list")
+        in2_list = load_list(in2, "in2_list")
+        gain = keep.tile([P, PACK], F32, name="gain")
+        nc.sync.dma_start(gain[:], gn.rearrange("(p t) o -> p (t o)", t=PACK))
+        tel_rows = [load_rows(tel, t, f"tel{t}") for t in range(PACK)]
+        w3_raw = load_weight(w3, "w3_raw")
+        slot_list = load_list(slot, "slot_list")
+        page = [load_rows(mem, t, f"page{t}") for t in range(PACK)]
+
+        def pick_scales(entries, name):
+            tile = keep.tile([P, S], U8, name=name, align_bytes=64)
+            nc.vector.tensor_copy(tile[:], table_scales[:].indirect(entries[:]))
+            return tile
+
+        def pick_words(entries, name):
+            tile = keep.tile([P, S], U32, name=name, align_bytes=64)
+            nc.vector.tensor_copy(tile[:], table_words[:].indirect(entries[:]))
+            return tile
+
+        def round_weight(raw, scalar_cols, name, tag):
+            dealt = keep.tile([P, PACK, P, PACK], BF16, name=name, tag=tag, align_bytes=64)
+            dst = dealt[:].rearrange("p t m j -> p m j t")
+            src = raw[:].rearrange("p j (m t) -> p m j t", t=PACK)
+            if scalar_cols > 0:
+                nc.scalar.copy(dst[:, :scalar_cols], src[:, :scalar_cols])
+            if scalar_cols < P:
+                nc.vector.tensor_copy(dst[:, scalar_cols:], src[:, scalar_cols:])
+            return dealt
+
+        def quantize_weight(dealt, calls, name):
+            codes = keep.tile([P, H], U32, name=name + "_codes", align_bytes=64)
+            scales = keep.tile([P, H], U8, name=name + "_scales", align_bytes=64)
+            flat = dealt[:].rearrange("p t m j -> p (t m j)")
+            width = H // calls
+            for i in range(calls):
+                cols = slice(i * width, (i + 1) * width)
+                nc.vector.quantize_mx(
+                    out=codes[:, cols].bitcast(FP8X4),
+                    scales=scales[:, cols],
+                    in_=flat[:, PACK * i * width : PACK * (i + 1) * width],
+                )
+            return codes, scales
+
+        def product(weight, t, words, scales, tag):
+            codes, wscales = weight
+            acc = psum.tile([P, words.shape[1]], F32, name=tag, tag=tag)
+            nc.tensor.matmul_mx(
+                out=acc[:],
+                lhsT=codes[:, t * P : (t + 1) * P].bitcast(FP8X4),
+                lhsT_scale=wscales[:, t * P : (t + 1) * P],
+                rhs=words[:].bitcast(FP8X4),
+                rhs_scale=scales[:],
+                start=True,
+                stop=True,
+            )
+            return acc
+
+        two_words = pick_words(two_list, "two_words")
+        offs_words = pick_words(offs_list, "offs_words")
+        two_scales = pick_scales(two_list, "two_scales")
+        offs_scales = pick_scales(offs_list, "offs_scales")
+
+        half_gain = keep.tile([P, PACK], F32, name="half_gain")
+        nc.gpsimd.tensor_scalar(half_gain[:], gain[:], 0.5, 0.0, ALU.mult, ALU.add)
+
+        w2_q = quantize_weight(round_weight(w2_raw, W2_SCALAR_COLS, "w2_dealt", "dealt"), 2, "w2")
+        w1_q = quantize_weight(round_weight(w1_raw, W1_SCALAR_COLS, "w1_dealt", "dealt"), PACK, "w1")
+
+        inverse = []
+        rank = []
+        sig = keep.tile([P, S], F32, name="sig", tag="sig", align_bytes=64)
+        for t in range(PACK):
+            degree = product(w2_q, t, two_words, two_scales, f"low{t % 2}")
+            rank.append(product(w1_q, t, offs_words, offs_scales, f"high{t}"))
+            nc.scalar.activation(sig[:], degree[:], ACT.Sigmoid, bias=-math.log(5.0), scale=-1.0)
+            inv = keep.tile([P, S], F32, name=f"inverse{t}")
+            nc.scalar.activation(inv[:], sig[:], ACT.Copy, bias=0.8, scale=3.2)
+            inverse.append(inv)
+        w3_dealt = round_weight(w3_raw, P, "w3_dealt", "sig")
+
+        share = [keep.tile([P, S], F32, name=f"share{t}") for t in range(PACK)]
+        first = {}
+        ring = [keep.tile([P, CW], F32, name=f"ring{i}") for i in range(2)]
+        summed = {}
+        z_rows = [keep.tile([P, PACK, CW], BF16, name=f"z_rows{c}", tag=f"z_rows{c}") for c in range(CHUNKS)]
+        accs = {}
+        results = {}
+
+        def make_share(t):
+            nc.vector.tensor_tensor(share[t][:], rank[t][:], inverse[t][:], ALU.mult)
+
+        def gather_first(t, c):
+            if (t, c) == (PACK - 1, 1):
+                first[t, c] = keep.tile([P, CW], F32, name="last_first", tag="woven0", align_bytes=64)
+            else:
+                first[t, c] = ring[t % 2]
+            nc.vector.tensor_tensor(
+                first[t, c][:],
+                share[t][:].indirect(in1_list[:, c * LW : (c + 1) * LW]),
+                tel_rows[t][:, c * CW : (c + 1) * CW],
+                ALU.add,
+            )
+
+        def gather_second(t, c):
+            summed[t, c] = keep.tile([P, CW], F32, name=f"summed{t}_{c}")
+            nc.vector.tensor_tensor(
+                summed[t, c][:],
+                share[t][:].indirect(in2_list[:, c * LW : (c + 1) * LW]),
+                first[t, c][:],
+                ALU.add,
+            )
+            nc.scalar.activation(z_rows[c][:, t, :], summed[t, c][:], ACT.Copy, scale=half_gain[:, t : t + 1])
+
+        def weave(c):
+            woven = keep.tile([P, CW, PACK], BF16, name=f"woven{c}", tag=f"woven{c}", align_bytes=64)
+            nc.scalar.copy(
+                woven[:].rearrange("p (g i) t -> p g t i", i=4),
+                z_rows[c][:].rearrange("p t (g i) -> p g t i", i=4),
+            )
+            return woven
+
+        def last_product(c, woven, w3_q):
+            z_codes = keep.tile([P, CW], U32, name=f"z_codes{c}", align_bytes=64)
+            z_scales = keep.tile([P, CW], U8, name=f"z_scales{c}", align_bytes=64)
+            nc.vector.quantize_mx(
+                out=z_codes[:].bitcast(FP8X4), scales=z_scales[:], in_=woven[:].rearrange("p s t -> p (s t)")
+            )
+            for t in range(PACK):
+                accs[t, c] = product(w3_q, t, z_codes, z_scales, ("low", "high")[c] + f"{t}")
+
+        def bring_out(t, c, tag):
+            results[t, c] = keep.tile([P, CW], F32, name=f"result{t}_{c}", tag=tag)
+            nc.scalar.copy(results[t, c][:], accs[t, c][:])
+
+        def put(t, c):
+            nc.vector.tensor_copy(page[t][:].indirect(slot_list[:, c * LW : (c + 1) * LW]), results[t, c][:])
+            if c + 1 == CHUNKS:
+                nc.sync.dma_start(out.rearrange("(p t) u -> p t u", t=PACK)[:, t, :], page[t][:])
+
+        make_share(0)
+        for t in range(PACK):
+            gather_first(t, 0)
+            if t + 1 < PACK:
+                make_share(t + 1)
+            else:
+                gather_first(0, 1)
+            gather_second(t, 0)
+        woven0 = weave(0)
+        gather_first(1, 1)
+        gather_second(0, 1)
+        w3_q = quantize_weight(w3_dealt, 1, "w3")
+        gather_first(2, 1)
+        gather_second(1, 1)
+        last_product(0, woven0, w3_q)
+        bring_out(0, 0, "result00")
+        bring_out(1, 0, "result10")
+        gather_first(3, 1)
+        gather_second(2, 1)
+        gather_second(3, 1)
+        woven1 = weave(1)
+        bring_out(2, 0, "z_rows1")
+        bring_out(3, 0, "result30")
+        put(0, 0)
+        put(1, 0)
+        last_product(1, woven1, w3_q)
+        for t in range(PACK):
+            bring_out(t, 1, f"result{t}1")
+        put(2, 0)
+        put(0, 1)
+        put(1, 1)
+        put(3, 0)
+        put(2, 1)
+        put(3, 1)

@@ -21,8 +21,8 @@ PACK = 4
 CHUNKS = 2
 CW = S // CHUNKS
 LW = CW // 16
-W2_SCALAR_COLS = 128
-W1_SCALAR_COLS = 32
+W2_SCALAR_COLS = 92
+W1_SCALAR_COLS = 44
 
 
 def tile_picked_rankstep_none_p_kernel(
@@ -40,32 +40,34 @@ def tile_picked_rankstep_none_p_kernel(
             return tile
 
         def load_weight(w, name):
-            raw = keep.tile([P, PACK, H], F32, name=name)
+            raw = keep.tile([P, PACK, H], F32, name=name, tag=name)
             nc.sync.dma_start(raw[:], w.rearrange("(p j) c -> p j c", j=PACK))
             return raw
 
         def load_rows(src, t, name):
-            tile = keep.tile([P, src.shape[1]], F32, name=name)
+            tile = keep.tile([P, src.shape[1]], F32, name=name, tag=name, align_bytes=64)
             nc.sync.dma_start(tile[:], src.rearrange("(p t) c -> p t c", t=PACK)[:, t, :])
             return tile
 
         table_scales = keep.tile([P, T], U8, name="table_scales")
-        nc.gpsimd.memset(table_scales[:].bitcast(I32), 0)
+        nc.vector.memset(table_scales[:].bitcast(I32), 0)
         two_list = load_list(two, "two_list")
         offs_list = load_list(offs, "offs_list")
+        table_words = keep.tile([P, T], U32, name="table_words")
+        words_in = x_words[0].rearrange("p c r -> p (c r)").bitcast(I32)
+        nc.sync.dma_start(table_words[:, : T // 2].bitcast(I32), words_in[:, : T // 2])
         for q in range(4):
-            nc.gpsimd.dma_start(
+            (nc.sync, nc.scalar)[q % 2].dma_start(
                 table_scales[32 * q : 32 * q + 4, :].bitcast(I32),
                 x_scales[0, 4 * q : 4 * q + 4, :].bitcast(I32),
             )
-        table_words = keep.tile([P, T], U32, name="table_words")
-        nc.sync.dma_start(table_words[:].bitcast(I32), x_words[0].rearrange("p c r -> p (c r)").bitcast(I32))
+        nc.sync.dma_start(table_words[:, T // 2 :].bitcast(I32), words_in[:, T // 2 :])
         w2_raw = load_weight(w2, "w2_raw")
         w1_raw = load_weight(w1, "w1_raw")
-        in1_list = load_list(in1, "in1_list")
-        in2_list = load_list(in2, "in2_list")
         gain = keep.tile([P, PACK], F32, name="gain")
         nc.sync.dma_start(gain[:], gn.rearrange("(p t) o -> p (t o)", t=PACK))
+        in1_list = load_list(in1, "in1_list")
+        in2_list = load_list(in2, "in2_list")
         tel_rows = [load_rows(tel, t, f"tel{t}") for t in range(PACK)]
         w3_raw = load_weight(w3, "w3_raw")
         slot_list = load_list(slot, "slot_list")
@@ -119,39 +121,41 @@ def tile_picked_rankstep_none_p_kernel(
             )
             return acc
 
-        two_words = pick_words(two_list, "two_words")
-        offs_words = pick_words(offs_list, "offs_words")
         two_scales = pick_scales(two_list, "two_scales")
         offs_scales = pick_scales(offs_list, "offs_scales")
+        two_words = pick_words(two_list, "two_words")
+        offs_words = pick_words(offs_list, "offs_words")
 
-        half_gain = keep.tile([P, PACK], F32, name="half_gain")
-        nc.gpsimd.tensor_scalar(half_gain[:], gain[:], 0.5, 0.0, ALU.mult, ALU.add)
+        warm = keep.tile([P, 2], F32, name="warm")
+        nc.gpsimd.memset(warm[:, 0:1], 0.0)
+        nc.scalar.activation(warm[:, 1:2], warm[:, 0:1], ACT.Sigmoid)
 
         w2_q = quantize_weight(round_weight(w2_raw, W2_SCALAR_COLS, "w2_dealt", "dealt"), 2, "w2")
         w1_q = quantize_weight(round_weight(w1_raw, W1_SCALAR_COLS, "w1_dealt", "dealt"), PACK, "w1")
 
-        inverse = []
-        rank = []
-        sig = keep.tile([P, S], F32, name="sig", tag="sig", align_bytes=64)
-        for t in range(PACK):
-            degree = product(w2_q, t, two_words, two_scales, f"low{t % 2}")
-            rank.append(product(w1_q, t, offs_words, offs_scales, f"high{t}"))
-            nc.scalar.activation(sig[:], degree[:], ACT.Sigmoid, bias=-math.log(5.0), scale=-1.0)
-            inv = keep.tile([P, S], F32, name=f"inverse{t}")
-            nc.scalar.activation(inv[:], sig[:], ACT.Copy, bias=0.8, scale=3.2)
-            inverse.append(inv)
-        w3_dealt = round_weight(w3_raw, P, "w3_dealt", "sig")
+        half_gain = keep.tile([P, PACK], F32, name="half_gain")
+        nc.scalar.mul(half_gain[:], gain[:], 1.6)
 
+        def scale_jump(t):
+            nc.scalar.mul(jump[:, t, :], tel_rows[t][:], 1.0 / 3.2)
+
+        jump = keep.tile([P, PACK, S], F32, name="jump", tag="dealt", align_bytes=64)
+        sigs = keep.tile([P, PACK, S], F32, name="sigs", tag="w1_raw")
         share = [keep.tile([P, S], F32, name=f"share{t}") for t in range(PACK)]
+
+        def make_share(t):
+            degree = product(w2_q, t, two_words, two_scales, f"bank{t}")
+            rank = product(w1_q, t, offs_words, offs_scales, f"bank{(t + 2) % PACK}")
+            nc.scalar.activation(sigs[:, t, :], degree[:], ACT.Sigmoid, bias=-math.log(5.0), scale=-1.0)
+            nc.vector.scalar_tensor_tensor(share[t][:], sigs[:, t, :], 0.25, rank[:], ALU.add, ALU.mult)
+            scale_jump(t)
+
         first = {}
         ring = [keep.tile([P, CW], F32, name=f"ring{i}") for i in range(2)]
         summed = {}
-        z_rows = [keep.tile([P, PACK, CW], BF16, name=f"z_rows{c}", tag=f"z_rows{c}") for c in range(CHUNKS)]
+        z_rows = {}
         accs = {}
         results = {}
-
-        def make_share(t):
-            nc.vector.tensor_tensor(share[t][:], rank[t][:], inverse[t][:], ALU.mult)
 
         def gather_first(t, c):
             if (t, c) == (PACK - 1, 1):
@@ -161,7 +165,7 @@ def tile_picked_rankstep_none_p_kernel(
             nc.vector.tensor_tensor(
                 first[t, c][:],
                 share[t][:].indirect(in1_list[:, c * LW : (c + 1) * LW]),
-                tel_rows[t][:, c * CW : (c + 1) * CW],
+                jump[:, t, c * CW : (c + 1) * CW],
                 ALU.add,
             )
 
@@ -173,6 +177,10 @@ def tile_picked_rankstep_none_p_kernel(
                 first[t, c][:],
                 ALU.add,
             )
+
+        def apply_gain(t, c):
+            if t == 0:
+                z_rows[c] = keep.tile([P, PACK, CW], BF16, name=f"z_rows{c}", tag=("w1_raw", "z_rows1")[c])
             nc.scalar.activation(z_rows[c][:, t, :], summed[t, c][:], ACT.Copy, scale=half_gain[:, t : t + 1])
 
         def weave(c):
@@ -190,7 +198,7 @@ def tile_picked_rankstep_none_p_kernel(
                 out=z_codes[:].bitcast(FP8X4), scales=z_scales[:], in_=woven[:].rearrange("p s t -> p (s t)")
             )
             for t in range(PACK):
-                accs[t, c] = product(w3_q, t, z_codes, z_scales, ("low", "high")[c] + f"{t}")
+                accs[t, c] = product(w3_q, t, z_codes, z_scales, f"bank{PACK * (1 - c) + t}")
 
         def bring_out(t, c, tag):
             results[t, c] = keep.tile([P, CW], F32, name=f"result{t}_{c}", tag=tag)
@@ -209,18 +217,25 @@ def tile_picked_rankstep_none_p_kernel(
             else:
                 gather_first(0, 1)
             gather_second(t, 0)
+        w3_dealt = round_weight(w3_raw, P, "w3_dealt", "tel3")
+        for t in range(PACK):
+            apply_gain(t, 0)
         woven0 = weave(0)
         gather_first(1, 1)
         gather_second(0, 1)
         w3_q = quantize_weight(w3_dealt, 1, "w3")
         gather_first(2, 1)
         gather_second(1, 1)
+        apply_gain(0, 1)
+        apply_gain(1, 1)
         last_product(0, woven0, w3_q)
         bring_out(0, 0, "result00")
         bring_out(1, 0, "result10")
         gather_first(3, 1)
         gather_second(2, 1)
         gather_second(3, 1)
+        apply_gain(2, 1)
+        apply_gain(3, 1)
         woven1 = weave(1)
         bring_out(2, 0, "z_rows1")
         bring_out(3, 0, "result30")

@@ -21,7 +21,7 @@ PACK = 4
 CHUNKS = 2
 CW = S // CHUNKS
 LW = CW // 16
-W2_SCALAR_COLS = 92
+W2_SCALAR_COLS = 52
 W1_SCALAR_COLS = 44
 
 
@@ -53,15 +53,13 @@ def tile_picked_rankstep_none_p_kernel(
         nc.vector.memset(table_scales[:].bitcast(I32), 0)
         two_list = load_list(two, "two_list")
         offs_list = load_list(offs, "offs_list")
-        table_words = keep.tile([P, T], U32, name="table_words")
-        words_in = x_words[0].rearrange("p c r -> p (c r)").bitcast(I32)
-        nc.sync.dma_start(table_words[:, : T // 2].bitcast(I32), words_in[:, : T // 2])
         for q in range(4):
-            (nc.sync, nc.scalar)[q % 2].dma_start(
+            nc.sync.dma_start(
                 table_scales[32 * q : 32 * q + 4, :].bitcast(I32),
                 x_scales[0, 4 * q : 4 * q + 4, :].bitcast(I32),
             )
-        nc.sync.dma_start(table_words[:, T // 2 :].bitcast(I32), words_in[:, T // 2 :])
+        table_words = keep.tile([P, T], U32, name="table_words")
+        nc.sync.dma_start(table_words[:].bitcast(I32), x_words[0].rearrange("p c r -> p (c r)").bitcast(I32))
         w2_raw = load_weight(w2, "w2_raw")
         w1_raw = load_weight(w1, "w1_raw")
         gain = keep.tile([P, PACK], F32, name="gain")

@@ -18,11 +18,14 @@ ALU = mybir.AluOpType
 
 P = 128
 PACK = 4
-CHUNKS = 2
-CW = S // CHUNKS
-LW = CW // 16
-W2_SCALAR_COLS = 52
-W1_SCALAR_COLS = 44
+QUADRANT = 32
+GROUP = 16
+HALVES = 2
+HALF = S // HALVES
+HALF_COLS = HALF // GROUP
+SHARE_SCALE = 1.6
+W2_SCALAR_ROWS = 52
+W1_SCALAR_ROWS = 44
 
 
 def tile_picked_rankstep_none_p_kernel(
@@ -35,7 +38,7 @@ def tile_picked_rankstep_none_p_kernel(
         psum = ctx.enter_context(tc.psum_pool(name="psum", bufs=1))
 
         def load_list(src, name):
-            tile = lists.tile([P, S // 16], U16, name=name)
+            tile = lists.tile([P, S // GROUP], U16, name=name)
             nc.sync.dma_start(tile[:], src)
             return tile
 
@@ -53,195 +56,176 @@ def tile_picked_rankstep_none_p_kernel(
         nc.vector.memset(table_scales[:].bitcast(I32), 0)
         two_list = load_list(two, "two_list")
         offs_list = load_list(offs, "offs_list")
-        for q in range(4):
+        for q in range(P // QUADRANT):
             nc.sync.dma_start(
-                table_scales[32 * q : 32 * q + 4, :].bitcast(I32),
+                table_scales[QUADRANT * q : QUADRANT * q + 4, :].bitcast(I32),
                 x_scales[0, 4 * q : 4 * q + 4, :].bitcast(I32),
             )
         table_words = keep.tile([P, T], U32, name="table_words")
         nc.sync.dma_start(table_words[:].bitcast(I32), x_words[0].rearrange("p c r -> p (c r)").bitcast(I32))
         w2_raw = load_weight(w2, "w2_raw")
         w1_raw = load_weight(w1, "w1_raw")
-        gain = keep.tile([P, PACK], F32, name="gain")
-        nc.sync.dma_start(gain[:], gn.rearrange("(p t) o -> p (t o)", t=PACK))
+        gn_rows = keep.tile([P, PACK], F32, name="gn_rows")
+        nc.sync.dma_start(gn_rows[:], gn.rearrange("(p t) o -> p (t o)", t=PACK))
         in1_list = load_list(in1, "in1_list")
         in2_list = load_list(in2, "in2_list")
         tel_rows = [load_rows(tel, t, f"tel{t}") for t in range(PACK)]
         w3_raw = load_weight(w3, "w3_raw")
         slot_list = load_list(slot, "slot_list")
-        page = [load_rows(mem, t, f"page{t}") for t in range(PACK)]
+        pages = [load_rows(mem, t, f"page{t}") for t in range(PACK)]
 
-        def pick_scales(entries, name):
-            tile = keep.tile([P, S], U8, name=name, align_bytes=64)
-            nc.vector.tensor_copy(tile[:], table_scales[:].indirect(entries[:]))
+        def pick(table, entries, dtype, name):
+            tile = keep.tile([P, S], dtype, name=name, align_bytes=64)
+            nc.vector.tensor_copy(tile[:], table[:].indirect(entries[:]))
             return tile
 
-        def pick_words(entries, name):
-            tile = keep.tile([P, S], U32, name=name, align_bytes=64)
-            nc.vector.tensor_copy(tile[:], table_words[:].indirect(entries[:]))
-            return tile
-
-        def round_weight(raw, scalar_cols, name, tag):
+        def round_weight(raw, scalar_rows, name, tag):
             dealt = keep.tile([P, PACK, P, PACK], BF16, name=name, tag=tag, align_bytes=64)
             dst = dealt[:].rearrange("p t m j -> p m j t")
             src = raw[:].rearrange("p j (m t) -> p m j t", t=PACK)
-            if scalar_cols > 0:
-                nc.scalar.copy(dst[:, :scalar_cols], src[:, :scalar_cols])
-            if scalar_cols < P:
-                nc.vector.tensor_copy(dst[:, scalar_cols:], src[:, scalar_cols:])
+            nc.scalar.copy(dst[:, :scalar_rows], src[:, :scalar_rows])
+            if scalar_rows < P:
+                nc.vector.tensor_copy(dst[:, scalar_rows:], src[:, scalar_rows:])
             return dealt
 
-        def quantize_weight(dealt, calls, name):
-            codes = keep.tile([P, H], U32, name=name + "_codes", align_bytes=64)
-            scales = keep.tile([P, H], U8, name=name + "_scales", align_bytes=64)
-            flat = dealt[:].rearrange("p t m j -> p (t m j)")
-            width = H // calls
+        def quantize(values, calls, name):
+            columns = values.shape[1] // PACK
+            words = keep.tile([P, columns], U32, name=name + "_words", align_bytes=64)
+            scales = keep.tile([P, columns], U8, name=name + "_scales", align_bytes=64)
+            width = columns // calls
             for i in range(calls):
                 cols = slice(i * width, (i + 1) * width)
                 nc.vector.quantize_mx(
-                    out=codes[:, cols].bitcast(FP8X4),
+                    out=words[:, cols].bitcast(FP8X4),
                     scales=scales[:, cols],
-                    in_=flat[:, PACK * i * width : PACK * (i + 1) * width],
+                    in_=values[:, PACK * i * width : PACK * (i + 1) * width],
                 )
-            return codes, scales
+            return words, scales
 
-        def product(weight, t, words, scales, tag):
-            codes, wscales = weight
-            acc = psum.tile([P, words.shape[1]], F32, name=tag, tag=tag)
+        def quantize_weight(dealt, calls, name):
+            return quantize(dealt[:].rearrange("p t m j -> p (t m j)"), calls, name)
+
+        def product(weight, t, moving, bank):
+            acc = psum.tile([P, moving[0].shape[1]], F32, name=f"bank{bank}", tag=f"bank{bank}")
             nc.tensor.matmul_mx(
                 out=acc[:],
-                lhsT=codes[:, t * P : (t + 1) * P].bitcast(FP8X4),
-                lhsT_scale=wscales[:, t * P : (t + 1) * P],
-                rhs=words[:].bitcast(FP8X4),
-                rhs_scale=scales[:],
+                lhsT=weight[0][:, t * P : (t + 1) * P].bitcast(FP8X4),
+                lhsT_scale=weight[1][:, t * P : (t + 1) * P],
+                rhs=moving[0][:].bitcast(FP8X4),
+                rhs_scale=moving[1][:],
                 start=True,
                 stop=True,
             )
             return acc
 
-        two_scales = pick_scales(two_list, "two_scales")
-        offs_scales = pick_scales(offs_list, "offs_scales")
-        two_words = pick_words(two_list, "two_words")
-        offs_words = pick_words(offs_list, "offs_words")
+        two_scales = pick(table_scales, two_list, U8, "two_scales")
+        offs_scales = pick(table_scales, offs_list, U8, "offs_scales")
+        two_words = pick(table_words, two_list, U32, "two_words")
+        offs_words = pick(table_words, offs_list, U32, "offs_words")
 
-        warm = keep.tile([P, 2], F32, name="warm")
-        nc.gpsimd.memset(warm[:, 0:1], 0.0)
-        nc.scalar.activation(warm[:, 1:2], warm[:, 0:1], ACT.Sigmoid)
+        w2_mx = quantize_weight(round_weight(w2_raw, W2_SCALAR_ROWS, "w2_dealt", "dealt"), 2, "w2")
+        w1_mx = quantize_weight(round_weight(w1_raw, W1_SCALAR_ROWS, "w1_dealt", "dealt"), PACK, "w1")
 
-        w2_q = quantize_weight(round_weight(w2_raw, W2_SCALAR_COLS, "w2_dealt", "dealt"), 2, "w2")
-        w1_q = quantize_weight(round_weight(w1_raw, W1_SCALAR_COLS, "w1_dealt", "dealt"), PACK, "w1")
-
-        half_gain = keep.tile([P, PACK], F32, name="half_gain")
-        nc.scalar.mul(half_gain[:], gain[:], 1.6)
-
-        def scale_jump(t):
-            nc.scalar.mul(jump[:, t, :], tel_rows[t][:], 1.0 / 3.2)
+        gain = keep.tile([P, PACK], F32, name="gain")
+        nc.scalar.mul(gain[:], gn_rows[:], 0.5 * SHARE_SCALE)
 
         jump = keep.tile([P, PACK, S], F32, name="jump", tag="dealt", align_bytes=64)
-        sigs = keep.tile([P, PACK, S], F32, name="sigs", tag="w1_raw")
-        share = [keep.tile([P, S], F32, name=f"share{t}") for t in range(PACK)]
+        tanhs = keep.tile([P, PACK, S], F32, name="tanhs", tag="w1_raw")
+        shares = [keep.tile([P, S], F32, name=f"share{t}") for t in range(PACK)]
 
         def make_share(t):
-            degree = product(w2_q, t, two_words, two_scales, f"bank{t}")
-            rank = product(w1_q, t, offs_words, offs_scales, f"bank{(t + 2) % PACK}")
-            nc.scalar.activation(sigs[:, t, :], degree[:], ACT.Sigmoid, bias=-math.log(5.0), scale=-1.0)
-            nc.vector.scalar_tensor_tensor(share[t][:], sigs[:, t, :], 0.25, rank[:], ALU.add, ALU.mult)
-            scale_jump(t)
+            degree = product(w2_mx, t, (two_words, two_scales), t)
+            rank = product(w1_mx, t, (offs_words, offs_scales), (t + 2) % PACK)
+            nc.scalar.activation(tanhs[:, t, :], degree[:], ACT.Tanh, bias=-0.5 * math.log(5.0), scale=-0.5)
+            nc.vector.scalar_tensor_tensor(shares[t][:], tanhs[:, t, :], 1.5, rank[:], ALU.add, ALU.mult)
+            nc.scalar.mul(jump[:, t, :], tel_rows[t][:], 1.0 / SHARE_SCALE)
 
-        first = {}
-        ring = [keep.tile([P, CW], F32, name=f"ring{i}") for i in range(2)]
+        partial = {}
+        ring = [keep.tile([P, HALF], F32, name=f"ring{i}") for i in range(2)]
         summed = {}
         z_rows = {}
         accs = {}
         results = {}
 
-        def gather_first(t, c):
-            if (t, c) == (PACK - 1, 1):
-                first[t, c] = keep.tile([P, CW], F32, name="last_first", tag="woven0", align_bytes=64)
-            else:
-                first[t, c] = ring[t % 2]
+        def list_half(entries, h):
+            return entries[:, h * HALF_COLS : (h + 1) * HALF_COLS]
+
+        def gather_in1(t, h, dst):
+            partial[t, h] = dst
             nc.vector.tensor_tensor(
-                first[t, c][:],
-                share[t][:].indirect(in1_list[:, c * LW : (c + 1) * LW]),
-                jump[:, t, c * CW : (c + 1) * CW],
-                ALU.add,
+                dst[:], shares[t][:].indirect(list_half(in1_list, h)), jump[:, t, h * HALF : (h + 1) * HALF], ALU.add
             )
 
-        def gather_second(t, c):
-            summed[t, c] = keep.tile([P, CW], F32, name=f"summed{t}_{c}")
+        def gather_in2(t, h):
+            summed[t, h] = keep.tile([P, HALF], F32, name=f"summed{t}_{h}")
             nc.vector.tensor_tensor(
-                summed[t, c][:],
-                share[t][:].indirect(in2_list[:, c * LW : (c + 1) * LW]),
-                first[t, c][:],
-                ALU.add,
+                summed[t, h][:], shares[t][:].indirect(list_half(in2_list, h)), partial[t, h][:], ALU.add
             )
 
-        def apply_gain(t, c):
-            if t == 0:
-                z_rows[c] = keep.tile([P, PACK, CW], BF16, name=f"z_rows{c}", tag=("w1_raw", "z_rows1")[c])
-            nc.scalar.activation(z_rows[c][:, t, :], summed[t, c][:], ACT.Copy, scale=half_gain[:, t : t + 1])
+        def apply_gain(t, h):
+            nc.scalar.activation(z_rows[h][:, t, :], summed[t, h][:], ACT.Copy, scale=gain[:, t : t + 1])
 
-        def weave(c):
-            woven = keep.tile([P, CW, PACK], BF16, name=f"woven{c}", tag=f"woven{c}", align_bytes=64)
+        def weave(h):
+            woven = keep.tile([P, HALF, PACK], BF16, name=f"woven{h}", tag=f"woven{h}", align_bytes=64)
             nc.scalar.copy(
                 woven[:].rearrange("p (g i) t -> p g t i", i=4),
-                z_rows[c][:].rearrange("p t (g i) -> p g t i", i=4),
+                z_rows[h][:].rearrange("p t (g i) -> p g t i", i=4),
             )
             return woven
 
-        def last_product(c, woven, w3_q):
-            z_codes = keep.tile([P, CW], U32, name=f"z_codes{c}", align_bytes=64)
-            z_scales = keep.tile([P, CW], U8, name=f"z_scales{c}", align_bytes=64)
-            nc.vector.quantize_mx(
-                out=z_codes[:].bitcast(FP8X4), scales=z_scales[:], in_=woven[:].rearrange("p s t -> p (s t)")
-            )
+        def last_product(h, woven, w3_mx):
+            z_mx = quantize(woven[:].rearrange("p s t -> p (s t)"), 1, f"z{h}")
             for t in range(PACK):
-                accs[t, c] = product(w3_q, t, z_codes, z_scales, f"bank{PACK * (1 - c) + t}")
+                accs[t, h] = product(w3_mx, t, z_mx, PACK * (1 - h) + t)
 
-        def bring_out(t, c, tag):
-            results[t, c] = keep.tile([P, CW], F32, name=f"result{t}_{c}", tag=tag)
-            nc.scalar.copy(results[t, c][:], accs[t, c][:])
+        def bring_out(t, h, tag):
+            results[t, h] = keep.tile([P, HALF], F32, name=f"result{t}_{h}", tag=tag)
+            nc.scalar.copy(results[t, h][:], accs[t, h][:])
 
-        def put(t, c):
-            nc.vector.tensor_copy(page[t][:].indirect(slot_list[:, c * LW : (c + 1) * LW]), results[t, c][:])
-            if c + 1 == CHUNKS:
-                nc.sync.dma_start(out.rearrange("(p t) u -> p t u", t=PACK)[:, t, :], page[t][:])
+        def put(t, h):
+            nc.vector.tensor_copy(pages[t][:].indirect(list_half(slot_list, h)), results[t, h][:])
+            if h + 1 == HALVES:
+                nc.sync.dma_start(out.rearrange("(p t) u -> p t u", t=PACK)[:, t, :], pages[t][:])
 
         make_share(0)
         for t in range(PACK):
-            gather_first(t, 0)
+            gather_in1(t, 0, ring[t % 2])
             if t + 1 < PACK:
                 make_share(t + 1)
             else:
-                gather_first(0, 1)
-            gather_second(t, 0)
-        w3_dealt = round_weight(w3_raw, P, "w3_dealt", "tel3")
+                gather_in1(0, 1, ring[0])
+            gather_in2(t, 0)
+        w3_dealt = round_weight(w3_raw, P, "w3_dealt", f"tel{PACK - 1}")
+        z_rows[0] = keep.tile([P, PACK, HALF], BF16, name="z_rows0", tag="w3_raw")
         for t in range(PACK):
             apply_gain(t, 0)
         woven0 = weave(0)
-        gather_first(1, 1)
-        gather_second(0, 1)
-        w3_q = quantize_weight(w3_dealt, 1, "w3")
-        gather_first(2, 1)
-        gather_second(1, 1)
+
+        gather_in1(1, 1, ring[1])
+        gather_in2(0, 1)
+        w3_mx = quantize_weight(w3_dealt, 1, "w3")
+        gather_in1(2, 1, ring[0])
+        gather_in2(1, 1)
+        z_rows[1] = keep.tile([P, PACK, HALF], BF16, name="z_rows1", tag="w3_raw")
         apply_gain(0, 1)
         apply_gain(1, 1)
-        last_product(0, woven0, w3_q)
-        bring_out(0, 0, "result00")
-        bring_out(1, 0, "result10")
-        gather_first(3, 1)
-        gather_second(2, 1)
-        gather_second(3, 1)
+        last_product(0, woven0, w3_mx)
+        bring_out(0, 0, "result0_0")
+        bring_out(1, 0, "result1_0")
+        gather_in1(3, 1, keep.tile([P, HALF], F32, name="last_partial", tag="woven0", align_bytes=64))
+        gather_in2(2, 1)
+        gather_in2(3, 1)
         apply_gain(2, 1)
         apply_gain(3, 1)
+
         woven1 = weave(1)
-        bring_out(2, 0, "z_rows1")
-        bring_out(3, 0, "result30")
+        bring_out(2, 0, "w3_raw")
+        bring_out(3, 0, "result3_0")
         put(0, 0)
         put(1, 0)
-        last_product(1, woven1, w3_q)
+        last_product(1, woven1, w3_mx)
         for t in range(PACK):
-            bring_out(t, 1, f"result{t}1")
+            bring_out(t, 1, f"result{t}_1")
         put(2, 0)
         put(0, 1)
         put(1, 1)

import math
from contextlib import ExitStack

import concourse.mybir as mybir

K, T, S, N, H, U = 512, 2048, 512, 512, 512, 1024
FLOPS = 2 * K * H * S * 2 + 2 * H * N * S

F32 = mybir.dt.float32
BF16 = mybir.dt.bfloat16
I32 = mybir.dt.int32
U32 = mybir.dt.uint32
U16 = mybir.dt.uint16
U8 = mybir.dt.uint8
FP8X4 = mybir.dt.float8_e4m3fn_x4
ACT = mybir.ActivationFunctionType
ALU = mybir.AluOpType

P = 128
PACK = 4
QUADRANT = 32
GROUP = 16
HALVES = 2
HALF = S // HALVES
HALF_COLS = HALF // GROUP
SHARE_SCALE = 1.6
W2_SCALAR_ROWS = 52
W1_SCALAR_ROWS = 44


def tile_picked_rankstep_none_p_kernel(
    tc, x_words, x_scales, w1, w2, tel, gn, w3, mem, offs, two, in1, in2, slot, out
):
    nc = tc.nc
    with ExitStack() as ctx:
        lists = ctx.enter_context(tc.tile_pool(name="lists", bufs=1))
        keep = ctx.enter_context(tc.tile_pool(name="keep", bufs=1))
        psum = ctx.enter_context(tc.psum_pool(name="psum", bufs=1))

        def load_list(src, name):
            tile = lists.tile([P, S // GROUP], U16, name=name)
            nc.sync.dma_start(tile[:], src)
            return tile

        def load_weight(w, name):
            raw = keep.tile([P, PACK, H], F32, name=name, tag=name)
            nc.sync.dma_start(raw[:], w.rearrange("(p j) c -> p j c", j=PACK))
            return raw

        def load_rows(src, t, name):
            tile = keep.tile([P, src.shape[1]], F32, name=name, tag=name, align_bytes=64)
            nc.sync.dma_start(tile[:], src.rearrange("(p t) c -> p t c", t=PACK)[:, t, :])
            return tile

        table_scales = keep.tile([P, T], U8, name="table_scales")
        nc.vector.memset(table_scales[:].bitcast(I32), 0)
        two_list = load_list(two, "two_list")
        offs_list = load_list(offs, "offs_list")
        for q in range(P // QUADRANT):
            nc.sync.dma_start(
                table_scales[QUADRANT * q : QUADRANT * q + 4, :].bitcast(I32),
                x_scales[0, 4 * q : 4 * q + 4, :].bitcast(I32),
            )
        table_words = keep.tile([P, T], U32, name="table_words")
        nc.sync.dma_start(table_words[:].bitcast(I32), x_words[0].rearrange("p c r -> p (c r)").bitcast(I32))
        w2_raw = load_weight(w2, "w2_raw")
        w1_raw = load_weight(w1, "w1_raw")
        gn_rows = keep.tile([P, PACK], F32, name="gn_rows")
        nc.sync.dma_start(gn_rows[:], gn.rearrange("(p t) o -> p (t o)", t=PACK))
        in1_list = load_list(in1, "in1_list")
        in2_list = load_list(in2, "in2_list")
        tel_rows = [load_rows(tel, t, f"tel{t}") for t in range(PACK)]
        w3_raw = load_weight(w3, "w3_raw")
        slot_list = load_list(slot, "slot_list")
        pages = [load_rows(mem, t, f"page{t}") for t in range(PACK)]

        def pick(table, entries, dtype, name):
            tile = keep.tile([P, S], dtype, name=name, align_bytes=64)
            nc.vector.tensor_copy(tile[:], table[:].indirect(entries[:]))
            return tile

        def round_weight(raw, scalar_rows, name, tag):
            dealt = keep.tile([P, PACK, P, PACK], BF16, name=name, tag=tag, align_bytes=64)
            dst = dealt[:].rearrange("p t m j -> p m j t")
            src = raw[:].rearrange("p j (m t) -> p m j t", t=PACK)
            nc.scalar.copy(dst[:, :scalar_rows], src[:, :scalar_rows])
            if scalar_rows < P:
                nc.vector.tensor_copy(dst[:, scalar_rows:], src[:, scalar_rows:])
            return dealt

        def quantize(values, calls, name):
            columns = values.shape[1] // PACK
            words = keep.tile([P, columns], U32, name=name + "_words", align_bytes=64)
            scales = keep.tile([P, columns], U8, name=name + "_scales", align_bytes=64)
            width = columns // calls
            for i in range(calls):
                cols = slice(i * width, (i + 1) * width)
                nc.vector.quantize_mx(
                    out=words[:, cols].bitcast(FP8X4),
                    scales=scales[:, cols],
                    in_=values[:, PACK * i * width : PACK * (i + 1) * width],
                )
            return words, scales

        def quantize_weight(dealt, calls, name):
            return quantize(dealt[:].rearrange("p t m j -> p (t m j)"), calls, name)

        def product(weight, t, moving, bank):
            acc = psum.tile([P, moving[0].shape[1]], F32, name=f"bank{bank}", tag=f"bank{bank}")
            nc.tensor.matmul_mx(
                out=acc[:],
                lhsT=weight[0][:, t * P : (t + 1) * P].bitcast(FP8X4),
                lhsT_scale=weight[1][:, t * P : (t + 1) * P],
                rhs=moving[0][:].bitcast(FP8X4),
                rhs_scale=moving[1][:],
                start=True,
                stop=True,
            )
            return acc

        two_scales = pick(table_scales, two_list, U8, "two_scales")
        offs_scales = pick(table_scales, offs_list, U8, "offs_scales")
        two_words = pick(table_words, two_list, U32, "two_words")
        offs_words = pick(table_words, offs_list, U32, "offs_words")

        w2_mx = quantize_weight(round_weight(w2_raw, W2_SCALAR_ROWS, "w2_dealt", "dealt"), 2, "w2")
        w1_mx = quantize_weight(round_weight(w1_raw, W1_SCALAR_ROWS, "w1_dealt", "dealt"), PACK, "w1")

        gain = keep.tile([P, PACK], F32, name="gain")
        nc.scalar.mul(gain[:], gn_rows[:], 0.5 * SHARE_SCALE)

        jump = keep.tile([P, PACK, S], F32, name="jump", tag="dealt", align_bytes=64)
        tanhs = keep.tile([P, PACK, S], F32, name="tanhs", tag="w1_raw")
        shares = [keep.tile([P, S], F32, name=f"share{t}") for t in range(PACK)]

        def make_share(t):
            degree = product(w2_mx, t, (two_words, two_scales), t)
            rank = product(w1_mx, t, (offs_words, offs_scales), (t + 2) % PACK)
            nc.scalar.activation(tanhs[:, t, :], degree[:], ACT.Tanh, bias=-0.5 * math.log(5.0), scale=-0.5)
            nc.vector.scalar_tensor_tensor(shares[t][:], tanhs[:, t, :], 1.5, rank[:], ALU.add, ALU.mult)
            nc.scalar.mul(jump[:, t, :], tel_rows[t][:], 1.0 / SHARE_SCALE)

        partial = {}
        ring = [keep.tile([P, HALF], F32, name=f"ring{i}") for i in range(2)]
        summed = {}
        z_rows = {}
        accs = {}
        results = {}

        def list_half(entries, h):
            return entries[:, h * HALF_COLS : (h + 1) * HALF_COLS]

        def gather_in1(t, h, dst):
            partial[t, h] = dst
            nc.vector.tensor_tensor(
                dst[:], shares[t][:].indirect(list_half(in1_list, h)), jump[:, t, h * HALF : (h + 1) * HALF], ALU.add
            )

        def gather_in2(t, h):
            summed[t, h] = keep.tile([P, HALF], F32, name=f"summed{t}_{h}")
            nc.vector.tensor_tensor(
                summed[t, h][:], shares[t][:].indirect(list_half(in2_list, h)), partial[t, h][:], ALU.add
            )

        def apply_gain(t, h):
            nc.scalar.activation(z_rows[h][:, t, :], summed[t, h][:], ACT.Copy, scale=gain[:, t : t + 1])

        def weave(h):
            woven = keep.tile([P, HALF, PACK], BF16, name=f"woven{h}", tag=f"woven{h}", align_bytes=64)
            nc.scalar.copy(
                woven[:].rearrange("p (g i) t -> p g t i", i=4),
                z_rows[h][:].rearrange("p t (g i) -> p g t i", i=4),
            )
            return woven

        def last_product(h, woven, w3_mx):
            z_mx = quantize(woven[:].rearrange("p s t -> p (s t)"), 1, f"z{h}")
            for t in range(PACK):
                accs[t, h] = product(w3_mx, t, z_mx, PACK * (1 - h) + t)

        def bring_out(t, h, tag):
            results[t, h] = keep.tile([P, HALF], F32, name=f"result{t}_{h}", tag=tag)
            nc.scalar.copy(results[t, h][:], accs[t, h][:])

        def put(t, h):
            nc.vector.tensor_copy(pages[t][:].indirect(list_half(slot_list, h)), results[t, h][:])
            if h + 1 == HALVES:
                nc.sync.dma_start(out.rearrange("(p t) u -> p t u", t=PACK)[:, t, :], pages[t][:])

        make_share(0)
        for t in range(PACK):
            gather_in1(t, 0, ring[t % 2])
            if t + 1 < PACK:
                make_share(t + 1)
            else:
                gather_in1(0, 1, ring[0])
            gather_in2(t, 0)
        w3_dealt = round_weight(w3_raw, P, "w3_dealt", f"tel{PACK - 1}")
        z_rows[0] = keep.tile([P, PACK, HALF], BF16, name="z_rows0", tag="w3_raw")
        for t in range(PACK):
            apply_gain(t, 0)
        woven0 = weave(0)

        gather_in1(1, 1, ring[1])
        gather_in2(0, 1)
        w3_mx = quantize_weight(w3_dealt, 1, "w3")
        gather_in1(2, 1, ring[0])
        gather_in2(1, 1)
        z_rows[1] = keep.tile([P, PACK, HALF], BF16, name="z_rows1", tag="w3_raw")
        apply_gain(0, 1)
        apply_gain(1, 1)
        last_product(0, woven0, w3_mx)
        bring_out(0, 0, "result0_0")
        bring_out(1, 0, "result1_0")
        gather_in1(3, 1, keep.tile([P, HALF], F32, name="last_partial", tag="woven0", align_bytes=64))
        gather_in2(2, 1)
        gather_in2(3, 1)
        apply_gain(2, 1)
        apply_gain(3, 1)

        woven1 = weave(1)
        bring_out(2, 0, "w3_raw")
        bring_out(3, 0, "result3_0")
        put(0, 0)
        put(1, 0)
        last_product(1, woven1, w3_mx)
        for t in range(PACK):
            bring_out(t, 1, f"result{t}_1")
        put(2, 0)
        put(0, 1)
        put(1, 1)
        put(3, 0)
        put(2, 1)
        put(3, 1)
